import numpy as np, ml_dtypes
CORES = [23,119,17,113]
N = 4
BF = ml_dtypes.bfloat16
def gentries(a):
    return np.ascontiguousarray(a.reshape(8, 16, -1).transpose(0, 2, 1)).reshape(8, -1)
def gtable(e):
    e = np.asarray(e); return np.ascontiguousarray(e.reshape(8, -1, 16).transpose(0, 2, 1)).reshape(128, -1).astype(np.int32)
L, T, B, RO = 2048, 4, 384, 2
W = L + T * B
def forest(rng, way):
    k = np.zeros((N, 8, RO, T, 2 * B), np.int64)
    for q in range(N):
        for g in range(8):
            for r in range(RO):
                free = np.ones(W, bool); m = int(way[q, g, r])
                for t in range(T):
                    pool = np.flatnonzero(free[:L + t * B])
                    if m == 0: p = rng.permutation(pool)[:2 * B]
                    elif m == 1: p = pool[:2 * B]
                    else: p = pool[len(pool) - 2 * B:]
                    if m > 0 and rng.random() < 0.5: p = rng.permutation(p)
                    free[p] = False; k[q, g, r, t] = p
    return k
def planned(rng, m, s):
    free = np.ones(W, bool); k = np.zeros((T, 2 * B), np.int64); order = rng.permutation(16); seq = None
    for t in range(T):
        pool = rng.permutation(np.flatnonzero(free[:L + t * B])); node = pool >= L; p = pool[:2 * B]
        if m == 0:
            late = node if t < 2 and t < T - 1 else ~node
            p = rng.permutation(pool[np.argsort(late, kind="stable")][:2 * B])
        elif m == 1 and t == 1:
            p = np.concatenate([pool[node], pool[~node][:B]])
        elif m == 2 and t == 1:
            p = np.concatenate([pool[~node][:B], pool[node]])
        elif m == 3:
            if t == 0:
                near = 128 * int(rng.integers(0, L // 128)) + rng.permutation(128); at = np.arange(2 * B)
                put = rng.permutation(np.flatnonzero(at % N == int(rng.integers(0, N))))[:128]
                rest = np.ones(2 * B, bool); rest[put] = False
                seq = np.zeros(2 * B, np.int64); seq[put] = near; seq[rest] = pool[~np.isin(pool, near)][:2 * B - 128]
            n = len(seq) // 2; slot = np.arange(n) if t == T - 1 else rng.permutation(B)[:n]
            p = np.zeros(2 * B, np.int64); rest = np.ones(2 * B, bool)
            rest[slot] = False; rest[B + slot] = False; p[slot] = seq[0::2]; p[B + slot] = seq[1::2]
            p[rest] = pool[~np.isin(pool, seq)][:2 * B - 2 * n]; seq = L + t * B + slot
        elif m == 4:
            two = np.isin(pool % 16, order[:2]); late = two if t < T - 1 else ~two
            p = rng.permutation(pool[np.argsort(late, kind="stable")][:2 * B])
        elif m == 5 and t == 0:
            p = rng.permutation(pool[np.argsort(order[pool % 16], kind="stable")][:2 * B])
        elif m == 6 and t == 0 and s is not None:
            p = p[np.argsort(s[p], kind="stable")]; i = rng.permutation(B); p = np.concatenate([p[:B][i], p[B:][i]])
        free[p] = False; k[t] = p
    return k
def parts(rng, way=None):
    x = rng.integers(-128, 128, (N, 8, 16, L)); k = forest(rng, np.zeros((N, 8, RO)) if way is None else way)
    a = rng.integers(-1, 2, (N, 8, 16, 16)); b = rng.integers(-1, 2, (N, 8, 16, 16)); w = rng.integers(-127, 128, (N, 8, 16))
    return x, k, a, b, w
def blocks(m):
    o = np.zeros((N, 8, 16, 8, 16), np.float32)
    for g in range(8): o[:, g, :, g, :] = m[:, g]
    return o.reshape(N, 128, 128).astype(BF)
def pack(x, k, a, b, w):
    return {"x": np.ascontiguousarray(x.reshape(N, 128, L)).astype(np.float32).astype(BF), "kids": np.stack([gtable(e.reshape(8, -1)) for e in k]),
            "ml": blocks(a), "mr": blocks(b), "w": w.reshape(N, 128, 1).astype(np.float32).astype(BF)}
def setup_inputs(rng):
    return pack(*parts(rng))
def setup_inputs_runs(rng):
    way = rng.choice(np.array([0, 1, 1, 2, 2]), (N, 8, RO)); i = rng.permutation(8); way[:, i[0]] = 1; way[:, i[1]] = 2
    return pack(*parts(rng, way))
def setup_inputs_ends(rng):
    x, k, a, b, w = parts(rng)
    x = rng.choice(np.array([-128, -127, -1, 0, 1, 126, 127]), (N, 8, 16, L))
    x[:, 0] = rng.integers(126, 128, (N, 16, L)); x[:, 1] = rng.integers(-128, -126, (N, 16, L)); a[:, :2] = 1; b[:, :2] = 1
    x[:, 2] = rng.choice(np.array([-128, 127]), (N, 1, L)); x[:, 2, 0] = rng.integers(-128, 128, (N, L)); a[:, 2] = 1; b[:, 2] = -1
    x[:, 3] = rng.integers(-2, 3, (N, 16, L))
    return pack(x, k, a, b, rng.choice(np.array([-127, 127]), (N, 8, 16)))
def setup_inputs_ties(rng):
    x, k, a, b, w = parts(rng)
    w[:, 0::4] = 0
    w[:, 1::4] = 0; w[:, 1::4, 0] = rng.integers(1, 128, (N, 2)); x[:, 1::4, 0] = rng.integers(-4, 5, (N, 2, L))
    for m in (a, b):
        m[:, 1::4, :, 0] = 0; m[:, 1::4, 0, 0] = 1
    v = rng.integers(-128, 128, (N, 2, 16, 1)); o = np.argsort(rng.random((N, 2, 16, L)), axis=2)
    x[:, 2::4] = np.take_along_axis(np.ascontiguousarray(np.broadcast_to(v, (N, 2, 16, L))), o, 2); w[:, 2::4] = rng.integers(1, 128, (N, 2, 1))
    x[:, 3::4, 2:] = 127; x[:, 3::4, 1] = rng.integers(-1, 2, (N, 2, L)); w[:, 3::4] = 127; w[:, 3::4, 0] = 0; w[:, 3::4, 1] = 1
    return pack(x, k, a, b, w)
def setup_inputs_crowd(rng):
    x, k, a, b, w = parts(rng); o = [int(g) for g in rng.permutation(8)]
    for i, v, c in ((2, 127, -1), (7, -127, 1)):
        x[:, o[i]] = np.where(rng.random((N, 1, L)) < 0.25, -128, rng.integers(-128, -99, (N, 16, L))); w[:, o[i]] = v; a[:, o[i]] = c; b[:, o[i]] = c
    w[:, o[3]] = 0
    for q in range(N):
        for i in range(8):
            s = np.add.reduce(w[q, o[i]][:, None] * x[q, o[i]], axis=0)
            for r in range(RO): k[q, o[i], r] = planned(rng, i if i < 7 else 1, s if r == 0 else None)
    return pack(x, k, a, b, w)
def setup_inputs_spread(rng):
    x, k, a, b, w = parts(rng)
    x = np.rint(127 * rng.uniform(-1, 1, (N, 8, 16, L)) * np.exp2(-rng.integers(0, 7, (N, 8, 1, L)).astype(np.float64))).astype(np.int64) * (rng.random((N, 8, 1, L)) > 0.0625)
    w = np.rint(127 * rng.uniform(-1, 1, (N, 8, 16)) * np.exp2(-rng.integers(0, 7, (N, 8, 16)).astype(np.float64))).astype(np.int64)
    s = rng.uniform(0.2, 1, (N, 8, 1, 1)); a = a * (rng.random(a.shape) < s); b = b * (rng.random(b.shape) < s)
    return pack(x, k, a, b, w)
def check_inputs(d):
    bad = []; own = np.kron(np.eye(8), np.ones((16, 16))) > 0
    for n, lo, hi in (("x", -128, 127), ("ml", -1, 1), ("mr", -1, 1), ("w", -127, 127)):
        v = np.asarray(d[n]).astype(np.float32)
        if not np.all((v == np.floor(v)) & (v >= lo) & (v <= hi)): bad.append("whole numbers of " + n)
        if n in ("ml", "mr") and not np.all(v[:, ~own] == 0): bad.append("zeros of " + n)
    k = np.stack([gentries(e) for e in d["kids"]]).astype(np.int64).reshape(N, 8, RO, T, 2 * B)
    for t in range(T):
        if np.min(k[:, :, :, t]) < 0 or np.max(k[:, :, :, t]) >= L + t * B: bad.append("range of kids")
    if not np.all(np.diff(np.sort(k.reshape(N, 8, RO, -1), axis=3), axis=3) > 0): bad.append("kids used twice")
    return bad
def reference(x, kids, ml, mr, w):
    leaf = x.astype(np.float64).reshape(N, 8, 16, L); ws = w.astype(np.float64).reshape(N, 8, 16, 1)
    cl, cr = [np.stack([m.astype(np.float64)[:, 16 * g:16 * g + 16, 16 * g:16 * g + 16] for g in range(8)], axis=1).transpose(0, 1, 3, 2) for m in (ml, mr)]
    kk = np.stack([gentries(e) for e in kids]).astype(np.int64).reshape(N, 8, RO, T, 2, B)
    for r in range(RO):
        h = np.zeros((N, 8, 16, W)); h[..., :L] = leaf
        size = np.ones((N, 8, W), np.int64); root = np.ones((N, 8, W), bool); order = []
        for t in range(T):
            a, b = kk[:, :, r, t, 0], kk[:, :, r, t, 1]; lo = L + t * B
            ha = np.take_along_axis(h, a[:, :, None, :], 3); hb = np.take_along_axis(h, b[:, :, None, :], 3)
            h[..., lo:lo + B] = np.clip(np.floor((np.matmul(cl, ha) + np.matmul(cr, hb)) * 0.25), -127, 127)
            size[..., lo:lo + B] = np.take_along_axis(size, a, 2) + np.take_along_axis(size, b, 2)
            swap = np.add.reduce(ws * ha, axis=2) < np.add.reduce(ws * hb, axis=2)
            np.put_along_axis(root, a, False, 2); np.put_along_axis(root, b, False, 2)
            order.append((np.where(swap, b, a), np.where(swap, a, b)))
        rs = np.where(root, size, 0); start = np.add.accumulate(rs, axis=2) - rs
        for t in range(T - 1, -1, -1):
            one, two = order[t]; s = start[..., L + t * B:L + t * B + B].copy()
            np.put_along_axis(start, one, s, 2); np.put_along_axis(start, two, s + np.take_along_axis(size, one, 2), 2)
        at = np.argsort(start[..., :L], axis=2)
        new = np.take_along_axis(leaf, at[:, :, None, :], 3).reshape(N, 8, 16, L // N, N)
        leaf = np.ascontiguousarray(new.transpose(4, 1, 2, 0, 3)).reshape(N, 8, 16, L)
    return {"y": leaf.reshape(N, 128, L).astype(np.float32).astype(BF)}

@@ -1,0 +1,504 @@
+from concourse.bass import DstId, RemoteDMATransfer
+from concourse.mybir import dt, AluOpType, ActivationFunctionType
+
+A = AluOpType
+AF = ActivationFunctionType
+L, NT, B, RO = 2048, 4, 384, 2
+K = 2 * B
+SLOT = 16
+EDGE = SLOT + 16 * 72
+TW = EDGE + NT * K
+MAGIC = 12582912.0
+PART = ((0, 48), (48, 128))
+
+SCRATCH = {
+    "KI": ("sbuf", [128, 384], "int32"), "K16": ("sbuf", [128, 384], "uint16"),
+    "ZA": ("sbuf", [128, 384], "int32"), "ZB": ("sbuf", [128, 384], "int32"), "SG": ("sbuf", [128, 384], "uint16"),
+    "VAL": ("sbuf", [128, NT * K], "float32"),
+    "ONES": ("sbuf", [128, 2048], "bfloat16"), "IDN": ("sbuf", [128, 128], "bfloat16"),
+    "BLA": ("sbuf", [128, 128], "bfloat16"), "BLK": ("sbuf", [128, 128], "bfloat16"), "TRI": ("sbuf", [128, 128], "bfloat16"),
+    "EQ": ("sbuf", [128, 2048], "bfloat16"), "DQ": ("sbuf", [128, 2048], "bfloat16"),
+    "PI": ("sbuf", [128, 8], "int32"), "QI": ("sbuf", [128, 8], "int32"), "QF": ("sbuf", [128, 8], "float32"),
+    "Q72": ("sbuf", [128, 8], "float32"),
+    "CI": ("sbuf", [128, 72], "float32"), "CT": ("sbuf", [128, 72], "float32"), "ZF": ("sbuf", [128, 224], "float32"),
+    "CB": ("sbuf", [128, 128], "bfloat16"),
+    "MLI": ("sbuf", [128, 128], "bfloat16"), "MRI": ("sbuf", [128, 128], "bfloat16"), "WI": ("sbuf", [128, 1], "bfloat16"),
+    "ML": ("sbuf", [128, 128], "bfloat16"), "MR": ("sbuf", [128, 128], "bfloat16"),
+    "WP": ("sbuf", [128, 128], "bfloat16"), "WN": ("sbuf", [128, 128], "bfloat16"),
+    "G0": ("sbuf", [128, K], "bfloat16"), "G1": ("sbuf", [128, K], "bfloat16"),
+    "F16": ("sbuf", [128, B], "float16"), "TM": ("sbuf", [128, 3 * B], "float32"), "DX": ("sbuf", [128, NT * K], "float32"),
+    "PR": ("sbuf", [128, 2048], "float16"), "QA": ("sbuf", [128, 128], "int32"), "QB": ("sbuf", [128, 128], "int32"),
+    "QL": ("sbuf", [128, 128], "uint16"),
+    "YL": ("sbuf", [128, L], "bfloat16"),
+}
+for _r in range(RO):
+    SCRATCH.update({
+        "H%d" % _r: ("sbuf", [128, L + 3 * B], "bfloat16"),
+        "PW%d" % _r: ("sbuf", [128, 4096], "float32"), "PL%d" % _r: ("sbuf", [128, 256], "float32"),
+        "NA%d" % _r: ("sbuf", [128, 72], "float32"), "PT%d" % _r: ("sbuf", [128, 200], "uint16"),
+        "RS%d" % _r: ("sbuf", [128, 224], "bfloat16"), "INC%d" % _r: ("sbuf", [128, 224], "float32"),
+        "RL%d" % _r: ("sbuf", [128, 224], "float16"), "RM%d" % _r: ("sbuf", [128, 128], "float16"),
+        "SZ%d" % _r: ("sbuf", [128, L + NT * B], "bfloat16"), "SR%d" % _r: ("sbuf", [128, 3 * K], "bfloat16"),
+        "TAB%d" % _r: ("sbuf", [128, TW], "float32"), "WB%d" % _r: ("sbuf", [128, L], "bfloat16"),
+    })
+for _b in range(8):
+    SCRATCH["b%d" % _b] = ("psum", [128, 512], "float32")
+PSUM = ["b%d" % i for i in range(8)]
+
+SEMAPHORES = ["qv", "qs", "qp", "qg", "sent", "arr0"] + ["arr1_%d" % i for i in range(4)] + ["d%d" % i for i in range(16)]
+
+
+def rank_program(g, core, T, topo):
+    me = T.rank_of(core)
+    if me is None:
+        return
+    cores = list(T.cores)
+    eng = {"v": g.vector, "s": g.scalar, "p": g.tensor, "g": g, "y": g.sync}
+    known = {q: {} for q in eng}
+    total = {}
+    acc = {}
+    ndma = [0]
+
+    def span(x):
+        if isinstance(x, str):
+            return x, 0, SCRATCH[x][1][1]
+        return x
+
+    def learn(q, sem, n, snap):
+        k = known[q]
+        if k.get(sem, 0) < n:
+            k[sem] = n
+        for s2, n2 in snap.items():
+            if k.get(s2, 0) < n2:
+                k[s2] = n2
+
+    def sync_for(q, reads, writes):
+        need = {}
+        for kind, lst in (("r", reads), ("w", writes)):
+            for x in lst:
+                b, lo, hi = span(x)
+                ps = b in PSUM
+                for rk, rlo, rhi, rq, sem, n, snap in acc.get(b, []):
+                    if ps:
+                        if rq == q and (q == "p" or (kind == "r" and rk == "r")):
+                            continue
+                    elif rhi <= lo or rlo >= hi or (kind == "r" and rk == "r"):
+                        continue
+                    if known[q].get(sem, 0) >= n:
+                        continue
+                    if sem not in need or need[sem][0] < n:
+                        need[sem] = (n, snap)
+        for sem in sorted(need, key=lambda s: -len(need[s][1])):
+            n, snap = need[sem]
+            if known[q].get(sem, 0) < n:
+                eng[q].wait_ge(T.sem[sem], n)
+                learn(q, sem, n, snap)
+
+    def note(q, reads, writes, sem, n):
+        snap = dict(known[q])
+        for kind, lst in (("r", reads), ("w", writes)):
+            for x in lst:
+                b, lo, hi = span(x)
+                old = acc.setdefault(b, [])
+                if kind == "w" and b not in PSUM:
+                    old[:] = [o for o in old if not (o[1] >= lo and o[2] <= hi)]
+                old.append((kind, lo, hi, q, sem, n, snap))
+
+    def op(q, reads, writes, call):
+        sync_for(q, reads, writes)
+        sem = "q" + q
+        total[sem] = total.get(sem, 0) + 1
+        call().then_inc(T.sem[sem], 1)
+        note(q, reads, writes, sem, total[sem])
+
+    def dma(q, reads, writes, out, in_):
+        sync_for(q, reads, writes)
+        sem = "d%d" % ndma[0]
+        ndma[0] += 1
+        total[sem] = 16
+        eng[q].dma_start(out=out, in_=in_).then_inc(T.sem[sem], 16)
+        note(q, reads, writes, sem, 16)
+
+    V, S, P = g.vector, g.scalar, g.tensor
+
+    def ts(b_out, lo, hi, in_ap, reads, s1, s2, o0, o1=None):
+        o = T[b_out][:, lo:hi]
+        if o1 is None:
+            op("v", reads, [(b_out, lo, hi)], lambda: V.tensor_scalar(o, in_ap, s1, None, o0))
+        else:
+            op("v", reads, [(b_out, lo, hi)], lambda: V.tensor_scalar(o, in_ap, s1, s2, o0, o1))
+
+    def tt(b_out, lo, hi, a0, a1, reads, o0):
+        op("v", reads, [(b_out, lo, hi)], lambda: V.tensor_tensor(T[b_out][:, lo:hi], a0, a1, o0))
+
+    def vcopy(b_out, lo, hi, in_ap, reads):
+        op("v", reads, [(b_out, lo, hi)], lambda: V.tensor_copy(T[b_out][:, lo:hi], in_ap))
+
+    def fill(b, lo, hi, c):
+        op("v", [], [(b, lo, hi)], lambda: V.memset(T[b][:, lo:hi], c))
+
+    def act(b_out, lo, hi, in_ap, reads, func, scale=None, bias=None):
+        o = T[b_out][:, lo:hi]
+        if bias is not None:
+            op("s", reads, [(b_out, lo, hi)], lambda: S.activation(o, in_ap, func, bias=bias, scale=scale))
+        elif scale is None:
+            op("s", reads, [(b_out, lo, hi)], lambda: S.activation(o, in_ap, func))
+        else:
+            op("s", reads, [(b_out, lo, hi)], lambda: S.activation(o, in_ap, func, scale=scale))
+
+    def copy(q, b_out, lo, hi, in_ap, reads):
+        if q == "v":
+            vcopy(b_out, lo, hi, in_ap, reads)
+        else:
+            act(b_out, lo, hi, in_ap, reads, AF.Copy)
+
+    def mm(bank, out_ap, lhs, lo, rhs_ap, reads, start, stop):
+        op("p", [(lhs, lo, lo + 128)] + reads, [bank], lambda: P.matmul(out_ap, T[lhs][:, lo:lo + 128], rhs_ap, start, stop))
+
+    def iota(b, lo, hi, pattern, base, cm, flag=True):
+        if flag:
+            op("g", [], [(b, lo, hi)], lambda: g.iota(T[b][:, lo:hi], pattern, base, cm, allow_small_or_imprecise_dtypes=True))
+        else:
+            op("g", [], [(b, lo, hi)], lambda: g.iota(T[b][:, lo:hi], pattern, base, cm))
+
+    def select(b_out, b_in, n, pattern, cmp, base, cm):
+        op("g", [(b_in, 0, n)], [(b_out, 0, n)], lambda: g.affine_select(T[b_out][:, 0:n], T[b_in][:, 0:n], pattern, cmp, 0.0, base, cm))
+
+    def lists(r):
+        lo, hi = 192 * r, 192 * r + 192
+        ki = T.KI[:, lo:hi]
+        ts("ZA", lo, hi, ki, [("KI", lo, hi)], 4097, None, A.mult)
+        vcopy("K16", lo, hi, ki, [("KI", lo, hi)])
+        ts("ZB", lo, hi, T.ZA[:, lo:hi], [("ZA", lo, hi)], 4, 4095, A.arith_shift_right, A.bitwise_and)
+        vcopy("SG", lo, hi, T.ZB[:, lo:hi], [("ZB", lo, hi)])
+
+    def scat(r, t):
+        b, c = "PW%d" % r, 192 * r + 48 * t
+        op("s", [("SG", c, c + 48), ("VAL", K * t, K * t + K)], [b],
+           lambda: S.activation(T[b][:, :].indirect(T.SG[:, c:c + 48]), T.VAL[:, K * t:K * t + K], AF.Silu))
+
+    def conv(r):
+        b, o = "PW%d" % r, "PL%d" % r
+        dma("y", [b], [o], T[o][:, :], T[b][0:128:16, :])
+
+    def size_gather(r, t, q):
+        sz, w, c, lo = "SZ%d" % r, L + B * t, 192 * r + 48 * t, K * (t - 1)
+        copy(q, "SR%d" % r, lo, lo + K, T[sz][:, 0:w].indirect(T.K16[:, c:c + 48]), [(sz, 0, w), ("K16", c, c + 48)])
+
+    def size_add(r, t):
+        sr, lo = "SR%d" % r, K * (t - 1)
+        for i in range(2):
+            c = lo + B * i
+            mm("b5", T.b5[:, 0:B], "IDN", 0, T[sr][:, c:c + B], [(sr, c, c + B)], i == 0, i == 1)
+
+    def size_store(r, t, q):
+        copy(q, "SZ%d" % r, L + B * t, L + B * t + B, T.b5[:, 0:B], ["b5"])
+
+    def size_list(r):
+        sz, c = "SZ%d" % r, L + B
+        for q in range(16):
+            mm("b4", T.b4[:, 0:72], "DQ", 128 * q, T[sz][:, c + q:c + 3 * B:16], [(sz, c, c + 3 * B)], q == 0, q == 15)
+
+    def root_sizes(r):
+        pl, rs, na = "PL%d" % r, "RS%d" % r, "NA%d" % r
+        ts(rs, 0, 224, T[pl][:, 0:224], [pl], 16.0, None, A.is_lt)
+        tt(na, 0, 72, T[rs][:, 128:200], T.CT[:, :], [(rs, 128, 200), "CT"], A.mult)
+        tt(rs, 152, 224, T[rs][:, 152:224], T.b4[:, 0:72], [(rs, 152, 224), "b4"], A.mult)
+        ts(rs, 128, 152, T[rs][:, 128:152], [(rs, 128, 152)], 2.0, None, A.mult)
+
+    def root_starts(r):
+        pl, rs, na, pt, inc, rl = ["%s%d" % (n, r) for n in ("PL", "RS", "NA", "PT", "INC", "RL")]
+        mm("b4", T.b4[:, 224:448], "BLK", 0, T[rs][:, :], [rs], True, True)
+        mm("b4", T.b4[:, 0:224], "TRI", 0, T[rs][:, :], [rs], True, True)
+        tt(pl, 128, 200, T[na][:, :], T[pl][:, 128:200], [na, (pl, 128, 200)], A.add)
+        op("v", ["b4", "ZF"], [inc], lambda: V.tensor_tensor_scan(T[inc][:, :], T.b4[:, 224:448], T.ZF[:, :], 0.0, A.add, A.add))
+        tt(rl, 0, 224, T[inc][:, :], T.b4[:, 0:224], [inc, "b4"], A.subtract)
+        ts(pt, 0, 200, T[pl][:, 0:200], [pl], 0.25, None, A.add)
+
+    def root_rows3(r):
+        rl = "RL%d" % r
+        for q in range(16):
+            mm("b6", T.b6[:, q:B:16], "EQ", 128 * q, T[rl][:, 200:224], [(rl, 200, 224)], True, True)
+
+    def root_rows(r, between):
+        rl, tab = "RL%d" % r, "TAB%d" % r
+        for bank, qs, e in (("b5", range(0, 6), "s"), ("b4", range(6, 12), "v"), ("b5", range(12, 16), "s")):
+            for i, q in enumerate(qs):
+                mm(bank, T[bank][:, 72 * i:72 * i + 72], "EQ", 128 * q, T[rl][:, 128:200], [(rl, 128, 200)], True, True)
+            c = SLOT + 72 * qs[0]
+            if between is not None and e == "v":
+                between()
+            copy(e, tab, c, c + 72 * len(qs), T[bank][:, 0:72 * len(qs)], [bank])
+
+    def root_leaves(r):
+        rl, rs = "RL%d" % r, "RS%d" % r
+        tt("RM%d" % r, 0, 128, T[rl][:, 0:128], T[rs][:, 0:128], [(rl, 0, 128), (rs, 0, 128)], A.mult)
+
+    def bias(t):
+        b = "b%d" % (t % 2)
+        mm(b, T[b][:, 0:B], "CB", 0, T.ONES[:, 0:B], [("ONES", 0, B)], True, False)
+
+    def gather(r, t, side, q):
+        h, w, c = "H%d" % r, L + B * t, 192 * r + 48 * t + 24 * side
+        copy(q, "G%d" % (t % 2), B * side, B * side + B, T[h][:, 0:w].indirect(T.K16[:, c:c + 24]), [(h, 0, w), ("K16", c, c + 24)])
+
+    def sums(t):
+        b, gb = "b%d" % (t % 2), "G%d" % (t % 2)
+        mm(b, T[b][:, 0:B], "ML", 0, T[gb][:, 0:B], [(gb, 0, B)], False, False)
+        mm(b, T[b][:, 0:B], "MR", 0, T[gb][:, B:K], [(gb, B, K)], False, True)
+
+    def dbank(t):
+        return "b2" if t % 2 == 0 else "b7"
+
+    def rbank(t):
+        return ("b3", "b3", "b0", "b1")[t]
+
+    def diff(t):
+        b, gb = dbank(t), "G%d" % (t % 2)
+        mm(b, T[b][:, 0:B], "WN", 0, T[gb][:, 0:B], [(gb, 0, B)], True, False)
+        mm(b, T[b][:, 0:B], "WP", 0, T[gb][:, B:K], [(gb, B, K)], False, True)
+
+    def vectors(r, t):
+        b, lo = "b%d" % (t % 2), L + B * t
+        ts("F16", 0, B, T[b][:, 0:B], [b], -127.0, 127.0, A.max, A.min)
+        ts("H%d" % r, lo, lo + B, T.F16[:, :], ["F16"], MAGIC, MAGIC, A.add, A.subtract)
+
+    def moves0():
+        ts("DX", 0, B, T.b2[:, 0:B], ["b2"], 0.0, None, A.is_gt)
+        ts("DX", B, K, T.b2[:, 0:B], ["b2"], 0.0, None, A.is_le)
+
+    def left_min(r, t):
+        b, sr, o = dbank(t), "SR%d" % r, K * (t - 1) + B
+        tt("TM", B * (t - 1), B * t, T[b][:, 0:B], T[sr][:, o:o + B], [b, (sr, o, o + B)], A.min)
+
+    def right_relu(t):
+        b = dbank(t)
+        act(rbank(t), 0, B, T[b][:, 0:B], [b], AF.Relu, -1.0, 16.0)
+
+    def left_relu(t):
+        act("DX", K * t, K * t + B, T.TM[:, B * (t - 1):B * t], [("TM", B * (t - 1), B * t)], AF.Relu)
+
+    def right_min(r, t):
+        b, sr, o = rbank(t), "SR%d" % r, K * (t - 1)
+        tt("DX", K * t + B, K * t + K, T[b][:, 0:B], T[sr][:, o:o + B], [b, (sr, o, o + B)], A.min)
+
+    def down(r):
+        tab, pt, h, wb, rm = ["%s%d" % (n, r) for n in ("TAB", "PT", "H", "WB", "RM")]
+        for i in (1, 0):
+            d = K * 3 + B * i
+            tt(tab, EDGE + B * i, EDGE + B * i + B, T.b6[:, 0:B], T.DX[:, d:d + B], ["b6", ("DX", d, d + B)], A.add)
+        for t in (2, 1, 0):
+            w = EDGE + K * (3 - t)
+            c = 128 + 24 * t
+            for i in range(2):
+                d = K * t + B * i
+                tt(tab, w + B * i, w + B * i + B, T[tab][:, 0:w].indirect(T[pt][:, c:c + 24]), T.DX[:, d:d + B],
+                   [(tab, 0, w), (pt, c, c + 24), ("DX", d, d + B)], A.add)
+        for k, (lo, hi) in enumerate(PART):
+            vcopy("PR", 16 * lo, 16 * hi, T[tab][:, :].indirect(T[pt][:, lo:hi]), [tab, (pt, lo, hi)])
+            b = "b%d" % (4 + k)
+            mm(b, T[b][:, 0:hi - lo], "IDN", 0, T[rm][:, lo:hi], [(rm, lo, hi)], True, False)
+            for q in range(16):
+                mm(b, T[b][:, 0:hi - lo], "DQ", 128 * q, T.PR[:, 16 * lo + q:16 * hi:16], [("PR", 16 * lo, 16 * hi)], False, q == 15)
+        for k, (lo, hi) in enumerate(PART):
+            b = "b%d" % (4 + k)
+            ts("QA", lo, hi, T[b][:, 0:hi - lo], [b], 2049.0, None, A.mult)
+            ts("QB", lo, hi, T.QA[:, lo:hi], [("QA", lo, hi)], 2, 2047, A.arith_shift_right, A.bitwise_and)
+            vcopy("QL", lo, hi, T.QB[:, lo:hi], [("QB", lo, hi)])
+            op("v", [("QL", lo, hi), (h, 16 * lo, 16 * hi)], [wb],
+               lambda: V.tensor_copy(T[wb][:, :].indirect(T.QL[:, lo:hi]), T[h][:, 16 * lo:16 * hi]))
+
+    def plan(src):
+        s = cores[src]
+        off = [d for d in range(4) if d != src and topo.chip(cores[d]) != topo.chip(s)]
+        on = [d for d in range(4) if d != src and topo.chip(cores[d]) == topo.chip(s)]
+        oe = topo.engines(s, cores[off[0]])
+        n = len(oe) // len(off)
+        res = {d: oe[n * i:n * i + n] for i, d in enumerate(off)}
+        for d in on:
+            res[d] = [e for e in topo.engines(s, cores[d]) if e not in oe]
+        return res
+
+    def exchange(r):
+        wb = "WB%d" % r
+        dst = ("H1", "YL")[r]
+        sem = "arr0" if r == 0 else "arr1_%d" % me
+        tr = []
+        n = 0
+        for d, es in plan(me).items():
+            rid, pid, _se = topo.addr(cores[d])
+            m = sum(1 << e for e in es)
+            n += len(es)
+            tr.append(RemoteDMATransfer(dst_ids=[DstId(rid=rid, pnc=pid)], dma_engine_mask=m, remote_sem=T.sem[sem],
+                                        src=T[wb][:, 512 * d:512 * d + 512], dst=T[dst][:, 512 * me:512 * me + 512]))
+        sync_for("g", [wb], [])
+        g.remote_dma_fused(tr, local_sem=T.sem["sent"])
+        total["sent"] = total.get("sent", 0) + n
+        note("g", [wb], [], "sent", total["sent"])
+        others = [s for s in range(4) if s != me]
+        got = sum(len(plan(s)[me]) for s in others)
+        for s in others:
+            sem, n = ("arr0", got) if r == 0 else ("arr1_%d" % s, len(plan(s)[me]))
+            total[sem] = n
+            acc.setdefault(dst, []).append(("w", 512 * s, 512 * s + 512, "x", sem, n, {}))
+        if r == 0:
+            vcopy(dst, 512 * me, 512 * me + 512, T[wb][:, 512 * me:512 * me + 512], [wb])
+
+    dma("y", [], [("KI", 0, 192)], T.KI[:, 0:192], T.kids[:, 0:192])
+    dma("s", [], [("H0", 0, L)], T.H0[:, 0:L], T.x[:, :])
+    dma("y", [], ["MLI"], T.MLI[:, :], T.ml[:, :])
+    dma("y", [], ["MRI"], T.MRI[:, :], T.mr[:, :])
+    dma("y", [], ["WI"], T.WI[:, :], T.w[:, :])
+    dma("y", [], [("KI", 192, 384)], T.KI[:, 192:384], T.kids[:, 192:384])
+
+    def val(t):
+        iota("VAL", K * t, K * t + K, [[1, K]], EDGE + K * (3 - t), 0)
+
+    fill("ONES", 0, 1280, 1.0)
+    for i in range(2):
+        act("PW0", 1536 + 1280 * i, 2816 + 1280 * i, T.ONES[:, 0:1280], [("ONES", 0, 1280)], AF.Copy, 0.0)
+    fill("PW0", 0, 1536, 0.0)
+    val(0)
+    select("BLA", "ONES", 128, [[-16, 8], [0, 16]], A.is_ge, 0, 1)
+    select("BLK", "BLA", 128, [[16, 8], [0, 16]], A.is_ge, 15, -1)
+    val(1)
+    select("IDN", "ONES", 128, [[-1, 128]], A.is_equal, 0, 1)
+    val(2)
+    val(3)
+    lists(0)
+    scat(0, 0)
+    fill("SZ0", 0, L, 1.0)
+    fill("SZ0", L, L + B, 2.0)
+    fill("CB", 0, 128, -0.375 / 128)
+    ts("ML", 0, 128, T.MLI[:, :], ["MLI"], 0.25, None, A.mult)
+    ts("MR", 0, 128, T.MRI[:, :], ["MRI"], 0.25, None, A.mult)
+    select("TRI", "BLK", 128, [[-1, 128]], A.is_ge, 0, 1)
+    iota("PI", 0, 8, [[0, 8]], 0, 1, False)
+    iota("CI", 0, 72, [[1, 72]], SLOT, 0)
+
+    scat(0, 1)
+    scat(0, 2)
+    scat(0, 3)
+    conv(0)
+    bias(0)
+    bias(1)
+    gather(0, 0, 0, "v")
+    gather(0, 0, 1, "v")
+    sums(0)
+    ts("WP", 0, 128, T.BLK[:, :], ["BLK", "WI"], T.WI[:, 0:1], 16.0, A.mult, A.mult)
+    ts("WN", 0, 128, T.BLK[:, :], ["BLK", "WI"], T.WI[:, 0:1], -16.0, A.mult, A.mult)
+    fill("ONES", 1280, 2048, 1.0)
+    select("EQ", "ONES", 2048, [[-1, 16], [-16, 8], [0, 16]], A.is_equal, 0, 1)
+    select("DQ", "EQ", 2048, [[1, 16], [0, 8], [-1, 16]], A.is_equal, 0, 0)
+    iota("PW1", 0, 4096, [[0, 4096]], 0, 0)
+    diff(0)
+    vectors(0, 0)
+    size_gather(0, 1, "v")
+    size_add(0, 1)
+    gather(0, 1, 0, "v")
+    gather(0, 1, 1, "v")
+    sums(1)
+    size_store(0, 1, "v")
+    moves0()
+    diff(1)
+    bias(2)
+    vectors(0, 1)
+    size_gather(0, 2, "v")
+    size_add(0, 2)
+    gather(0, 2, 0, "v")
+    gather(0, 2, 1, "v")
+    sums(2)
+    size_store(0, 2, "v")
+    diff(2)
+    size_gather(0, 3, "s")
+    size_add(0, 3)
+    ts("QI", 0, 8, T.PI[:, :], ["PI"], 15, None, A.bitwise_and)
+    fill("ZF", 0, 224, 0.0)
+    vectors(0, 2)
+    right_relu(1)
+    size_store(0, 3, "s")
+    size_list(0)
+    gather(0, 3, 0, "v")
+    gather(0, 3, 1, "v")
+    vcopy("QF", 0, 8, T.QI[:, :], ["QI"])
+    fill("TAB0", 0, 16, 0.0)
+    ts("Q72", 0, 8, T.QF[:, :], ["QF"], 72.0, None, A.mult)
+    fill("TAB1", 0, 16, 0.0)
+    ts("CT", 0, 72, T.CI[:, :], ["CI", "Q72"], T.Q72[:, 0:1], None, A.add)
+    left_min(0, 1)
+    left_relu(1)
+    right_min(0, 1)
+    left_min(0, 2)
+    right_relu(2)
+    left_relu(2)
+    root_sizes(0)
+    right_min(0, 2)
+    diff(3)
+    root_starts(0)
+    left_min(0, 3)
+    right_relu(3)
+    left_relu(3)
+    right_min(0, 3)
+    root_rows3(0)
+    root_rows(0, lambda: (lists(1), fill("SZ1", 0, L, 1.0), fill("SZ1", L, L + B, 2.0)))
+    root_leaves(0)
+    size_gather(1, 1, "s")
+    scat(1, 0)
+    size_add(1, 1)
+    size_store(1, 1, "s")
+    size_gather(1, 2, "s")
+    scat(1, 1)
+    scat(1, 2)
+    scat(1, 3)
+    conv(1)
+    down(0)
+    size_add(1, 2)
+    size_store(1, 2, "s")
+    size_gather(1, 3, "s")
+    size_add(1, 3)
+    size_store(1, 3, "s")
+    exchange(0)
+    size_list(1)
+    root_sizes(1)
+    root_starts(1)
+    bias(0)
+    bias(1)
+    root_rows3(1)
+    root_rows(1, None)
+    root_leaves(1)
+
+    for t in range(NT):
+        gather(1, t, 0, "v")
+        gather(1, t, 1, "s")
+        if t < 3:
+            sums(t)
+        if t == 1:
+            moves0()
+        if t == 2:
+            left_min(1, 1)
+            right_relu(1)
+            left_relu(1)
+        if t == 3:
+            right_relu(2)
+            right_min(1, 1)
+            left_min(1, 2)
+        diff(t)
+        if t == 1:
+            bias(2)
+        if t < 3:
+            vectors(1, t)
+    right_min(1, 2)
+    right_relu(3)
+    left_min(1, 3)
+    left_relu(3)
+    left_relu(2)
+    right_min(1, 3)
+    down(1)
+    exchange(1)
+    dma("s", [("WB1", 512 * me, 512 * me + 512)], [], T.y[:, 512 * me:512 * me + 512], T.WB1[:, 512 * me:512 * me + 512])
+    for i, s in enumerate([s for s in range(4) if topo.chip(cores[s]) == topo.chip(core) and s != me] +
+                          [s for s in range(4) if topo.chip(cores[s]) != topo.chip(core)]):
+        dma("ysy"[i], [("YL", 512 * s, 512 * s + 512)], [], T.y[:, 512 * s:512 * s + 512], T.YL[:, 512 * s:512 * s + 512])
+    for sem in sorted(total):
+        if known["g"].get(sem, 0) < total[sem]:
+            g.wait_ge(T.sem[sem], total[sem])

@@ -5,32 +5,33 @@ A = AluOpType
 AF = ActivationFunctionType
 L, NT, B, RO = 2048, 4, 384, 2
 K = 2 * B
+C = B // 2
 SLOT = 16
 EDGE = SLOT + 16 * 72
 TW = EDGE + NT * K
 MAGIC = 12582912.0
-PART = ((0, 48), (48, 128))
+PART = ((0, 64), (64, 128))
 
 SCRATCH = {
     "KI": ("sbuf", [128, 384], "int32"), "K16": ("sbuf", [128, 384], "uint16"),
     "ZA": ("sbuf", [128, 384], "int32"), "ZB": ("sbuf", [128, 384], "int32"), "SG": ("sbuf", [128, 384], "uint16"),
-    "VAL": ("sbuf", [128, NT * K], "float32"),
-    "ONES": ("sbuf", [128, 2048], "bfloat16"), "IDN": ("sbuf", [128, 128], "bfloat16"),
+    "VAL": ("sbuf", [128, NT * K], "float32"), "ZZ": ("sbuf", [128, 256], "float32"),
+    "SZ": ("sbuf", [128, L + NT * B], "bfloat16"), "TAB": ("sbuf", [128, TW], "float32"),
+    "IDN": ("sbuf", [128, 128], "bfloat16"), "NID": ("sbuf", [128, 128], "bfloat16"),
     "BLA": ("sbuf", [128, 128], "bfloat16"), "BLK": ("sbuf", [128, 128], "bfloat16"), "TRI": ("sbuf", [128, 128], "bfloat16"),
     "EQ": ("sbuf", [128, 2048], "bfloat16"), "DQ": ("sbuf", [128, 2048], "bfloat16"),
-    "PI": ("sbuf", [128, 8], "int32"), "QI": ("sbuf", [128, 8], "int32"), "QF": ("sbuf", [128, 8], "float32"),
-    "Q72": ("sbuf", [128, 8], "float32"),
-    "CI": ("sbuf", [128, 72], "float32"), "CT": ("sbuf", [128, 72], "float32"), "ZF": ("sbuf", [128, 224], "float32"),
+    "C72": ("sbuf", [128, 16], "bfloat16"), "CI": ("sbuf", [128, 72], "float32"), "CT": ("sbuf", [128, 72], "float32"),
     "CB": ("sbuf", [128, 128], "bfloat16"),
-    "MLI": ("sbuf", [128, 128], "bfloat16"), "MRI": ("sbuf", [128, 128], "bfloat16"), "WI": ("sbuf", [128, 1], "bfloat16"),
-    "ML": ("sbuf", [128, 128], "bfloat16"), "MR": ("sbuf", [128, 128], "bfloat16"),
+    "MI": ("sbuf", [128, 256], "bfloat16"), "WI": ("sbuf", [128, 1], "bfloat16"), "MM": ("sbuf", [128, 256], "bfloat16"),
     "WP": ("sbuf", [128, 128], "bfloat16"), "WN": ("sbuf", [128, 128], "bfloat16"),
-    "G0": ("sbuf", [128, K], "bfloat16"), "G1": ("sbuf", [128, K], "bfloat16"),
-    "F16": ("sbuf", [128, B], "float16"), "TM": ("sbuf", [128, 3 * B], "float32"), "DX": ("sbuf", [128, NT * K], "float32"),
+    "F16": ("sbuf", [128, B], "float16"), "DX": ("sbuf", [128, NT * K], "float32"),
+    "UX": ("sbuf", [128, B], "float32"), "UB": ("sbuf", [128, K], "bfloat16"),
     "PR": ("sbuf", [128, 2048], "float16"), "QA": ("sbuf", [128, 128], "int32"), "QB": ("sbuf", [128, 128], "int32"),
     "QL": ("sbuf", [128, 128], "uint16"),
     "YL": ("sbuf", [128, L], "bfloat16"),
 }
+for _t in range(NT):
+    SCRATCH["G%d" % _t] = ("sbuf", [128, K], "bfloat16")
 for _r in range(RO):
     SCRATCH.update({
         "H%d" % _r: ("sbuf", [128, L + 3 * B], "bfloat16"),
@@ -38,8 +39,7 @@ for _r in range(RO):
         "NA%d" % _r: ("sbuf", [128, 72], "float32"), "PT%d" % _r: ("sbuf", [128, 200], "uint16"),
         "RS%d" % _r: ("sbuf", [128, 224], "bfloat16"), "INC%d" % _r: ("sbuf", [128, 224], "float32"),
         "RL%d" % _r: ("sbuf", [128, 224], "float16"), "RM%d" % _r: ("sbuf", [128, 128], "float16"),
-        "SZ%d" % _r: ("sbuf", [128, L + NT * B], "bfloat16"), "SR%d" % _r: ("sbuf", [128, 3 * K], "bfloat16"),
-        "TAB%d" % _r: ("sbuf", [128, TW], "float32"), "WB%d" % _r: ("sbuf", [128, L], "bfloat16"),
+        "SR%d" % _r: ("sbuf", [128, 3 * K], "bfloat16"), "WB%d" % _r: ("sbuf", [128, L], "bfloat16"),
     })
 for _b in range(8):
     SCRATCH["b%d" % _b] = ("psum", [128, 512], "float32")
@@ -182,8 +182,8 @@ def rank_program(g, core, T, topo):
         dma("y", [b], [o], T[o][:, :], T[b][0:128:16, :])
 
     def size_gather(r, t, q):
-        sz, w, c, lo = "SZ%d" % r, L + B * t, 192 * r + 48 * t, K * (t - 1)
-        copy(q, "SR%d" % r, lo, lo + K, T[sz][:, 0:w].indirect(T.K16[:, c:c + 48]), [(sz, 0, w), ("K16", c, c + 48)])
+        w, c, lo = L + B * t, 192 * r + 48 * t, K * (t - 1)
+        copy(q, "SR%d" % r, lo, lo + K, T.SZ[:, 0:w].indirect(T.K16[:, c:c + 48]), [("SZ", 0, w), ("K16", c, c + 48)])
 
     def size_add(r, t):
         sr, lo = "SR%d" % r, K * (t - 1)
@@ -192,27 +192,28 @@ def rank_program(g, core, T, topo):
             mm("b5", T.b5[:, 0:B], "IDN", 0, T[sr][:, c:c + B], [(sr, c, c + B)], i == 0, i == 1)
 
     def size_store(r, t, q):
-        copy(q, "SZ%d" % r, L + B * t, L + B * t + B, T.b5[:, 0:B], ["b5"])
+        copy(q, "SZ", L + B * t, L + B * t + B, T.b5[:, 0:B], ["b5"])
 
     def size_list(r):
-        sz, c = "SZ%d" % r, L + B
         for q in range(16):
-            mm("b4", T.b4[:, 0:72], "DQ", 128 * q, T[sz][:, c + q:c + 3 * B:16], [(sz, c, c + 3 * B)], q == 0, q == 15)
+            mm("b6", T.b6[:, 0:96], "DQ", 128 * q, T.SZ[:, L + q:L + 4 * B:16], [("SZ", L, L + 4 * B)], q == 0, q == 15)
+
+    def root_flags(r):
+        pl, rs = "PL%d" % r, "RS%d" % r
+        act(rs, 0, 224, T[pl][:, 0:224], [pl], AF.Relu, -1.0, 1.0)
 
     def root_sizes(r):
-        pl, rs, na = "PL%d" % r, "RS%d" % r, "NA%d" % r
-        ts(rs, 0, 224, T[pl][:, 0:224], [pl], 16.0, None, A.is_lt)
+        rs, na = "RS%d" % r, "NA%d" % r
         tt(na, 0, 72, T[rs][:, 128:200], T.CT[:, :], [(rs, 128, 200), "CT"], A.mult)
-        tt(rs, 152, 224, T[rs][:, 152:224], T.b4[:, 0:72], [(rs, 152, 224), "b4"], A.mult)
-        ts(rs, 128, 152, T[rs][:, 128:152], [(rs, 128, 152)], 2.0, None, A.mult)
+        tt(rs, 128, 224, T[rs][:, 128:224], T.b6[:, 0:96], [(rs, 128, 224), "b6"], A.mult)
 
     def root_starts(r):
         pl, rs, na, pt, inc, rl = ["%s%d" % (n, r) for n in ("PL", "RS", "NA", "PT", "INC", "RL")]
-        mm("b4", T.b4[:, 224:448], "BLK", 0, T[rs][:, :], [rs], True, True)
-        mm("b4", T.b4[:, 0:224], "TRI", 0, T[rs][:, :], [rs], True, True)
+        mm("b6", T.b6[:, 224:448], "BLK", 0, T[rs][:, :], [rs], True, True)
+        mm("b6", T.b6[:, 0:224], "TRI", 0, T[rs][:, :], [rs], True, True)
         tt(pl, 128, 200, T[na][:, :], T[pl][:, 128:200], [na, (pl, 128, 200)], A.add)
-        op("v", ["b4", "ZF"], [inc], lambda: V.tensor_tensor_scan(T[inc][:, :], T.b4[:, 224:448], T.ZF[:, :], 0.0, A.add, A.add))
-        tt(rl, 0, 224, T[inc][:, :], T.b4[:, 0:224], [inc, "b4"], A.subtract)
+        op("v", ["b6", rs], [inc], lambda: V.tensor_tensor_scan(T[inc][:, :], T.b6[:, 224:448], T[rs][:, :], 0.0, A.add, A.max))
+        tt(rl, 0, 224, T[inc][:, :], T.b6[:, 0:224], [inc, "b6"], A.subtract)
         ts(pt, 0, 200, T[pl][:, 0:200], [pl], 0.25, None, A.add)
 
     def root_rows3(r):
@@ -220,70 +221,93 @@ def rank_program(g, core, T, topo):
         for q in range(16):
             mm("b6", T.b6[:, q:B:16], "EQ", 128 * q, T[rl][:, 200:224], [(rl, 200, 224)], True, True)
 
-    def root_rows(r, between):
-        rl, tab = "RL%d" % r, "TAB%d" % r
-        for bank, qs, e in (("b5", range(0, 6), "s"), ("b4", range(6, 12), "v"), ("b5", range(12, 16), "s")):
+    def root_rows(r, es):
+        rl = "RL%d" % r
+        for bank, qs, e in (("b5", range(0, 6), es[0]), ("b4", range(6, 12), es[1]), ("b2", range(12, 16), es[2])):
             for i, q in enumerate(qs):
                 mm(bank, T[bank][:, 72 * i:72 * i + 72], "EQ", 128 * q, T[rl][:, 128:200], [(rl, 128, 200)], True, True)
             c = SLOT + 72 * qs[0]
-            if between is not None and e == "v":
-                between()
-            copy(e, tab, c, c + 72 * len(qs), T[bank][:, 0:72 * len(qs)], [bank])
+            copy(e, "TAB", c, c + 72 * len(qs), T[bank][:, 0:72 * len(qs)], [bank])
+            if bank == "b5":
+                root_rows3(r)
 
     def root_leaves(r):
         rl, rs = "RL%d" % r, "RS%d" % r
         tt("RM%d" % r, 0, 128, T[rl][:, 0:128], T[rs][:, 0:128], [(rl, 0, 128), (rs, 0, 128)], A.mult)
 
-    def bias(t):
-        b = "b%d" % (t % 2)
-        mm(b, T[b][:, 0:B], "CB", 0, T.ONES[:, 0:B], [("ONES", 0, B)], True, False)
+    def bias():
+        for b in ("b0", "b1"):
+            mm(b, T[b][:, 0:C], "CB", 0, T.SZ[:, 0:C], [("SZ", 0, C)], True, False)
 
-    def gather(r, t, side, q):
-        h, w, c = "H%d" % r, L + B * t, 192 * r + 48 * t + 24 * side
-        copy(q, "G%d" % (t % 2), B * side, B * side + B, T[h][:, 0:w].indirect(T.K16[:, c:c + 24]), [(h, 0, w), ("K16", c, c + 24)])
+    def gather(r, t, side, h, q):
+        hb, w, c, o = "H%d" % r, L + B * t, 192 * r + 48 * t + 24 * side + 12 * h, B * side + C * h
+        copy(q, "G%d" % t, o, o + C, T[hb][:, 0:w].indirect(T.K16[:, c:c + 12]), [(hb, 0, w), ("K16", c, c + 12)])
 
     def sums(t):
-        b, gb = "b%d" % (t % 2), "G%d" % (t % 2)
-        mm(b, T[b][:, 0:B], "ML", 0, T[gb][:, 0:B], [(gb, 0, B)], False, False)
-        mm(b, T[b][:, 0:B], "MR", 0, T[gb][:, B:K], [(gb, B, K)], False, True)
+        gb = "G%d" % t
+        for h, b in enumerate(("b0", "b1")):
+            for side in range(2):
+                o = B * side + C * h
+                mm(b, T[b][:, 0:C], "MM", 128 * side, T[gb][:, o:o + C], [(gb, o, o + C)], False, side == 1)
 
     def dbank(t):
-        return "b2" if t % 2 == 0 else "b7"
+        return ("b2", "b7", "b4", "b0")[t]
 
     def rbank(t):
-        return ("b3", "b3", "b0", "b1")[t]
+        return ("b3", "b3", "b1", "b3")[t]
 
     def diff(t):
-        b, gb = dbank(t), "G%d" % (t % 2)
+        b, gb = dbank(t), "G%d" % t
         mm(b, T[b][:, 0:B], "WN", 0, T[gb][:, 0:B], [(gb, 0, B)], True, False)
         mm(b, T[b][:, 0:B], "WP", 0, T[gb][:, B:K], [(gb, B, K)], False, True)
 
     def vectors(r, t):
-        b, lo = "b%d" % (t % 2), L + B * t
-        ts("F16", 0, B, T[b][:, 0:B], [b], -127.0, 127.0, A.max, A.min)
-        ts("H%d" % r, lo, lo + B, T.F16[:, :], ["F16"], MAGIC, MAGIC, A.add, A.subtract)
+        for h, b in enumerate(("b0", "b1")):
+            ts("F16", C * h, C * h + C, T[b][:, 0:C], [b], -127.0, 127.0, A.max, A.min)
+        for h in range(2):
+            lo = L + B * t + C * h
+            ts("H%d" % r, lo, lo + C, T.F16[:, C * h:C * h + C], [("F16", C * h, C * h + C)], MAGIC, MAGIC, A.add, A.subtract)
 
-    def moves0():
-        ts("DX", 0, B, T.b2[:, 0:B], ["b2"], 0.0, None, A.is_gt)
-        ts("DX", B, K, T.b2[:, 0:B], ["b2"], 0.0, None, A.is_le)
+    def moves0_a():
+        act("UX", 0, B, T.b2[:, 0:B], ["b2"], AF.Relu, -1.0, 1.0)
 
-    def left_min(r, t):
-        b, sr, o = dbank(t), "SR%d" % r, K * (t - 1) + B
-        tt("TM", B * (t - 1), B * t, T[b][:, 0:B], T[sr][:, o:o + B], [b, (sr, o, o + B)], A.min)
+    def moves0_b():
+        act("DX", 0, B, T.UX[:, 0:B], [("UX", 0, B)], AF.Relu, -1.0, 1.0)
+        act("DX", B, K, T.DX[:, 0:B], [("DX", 0, B)], AF.Relu, -1.0, 1.0)
 
-    def right_relu(t):
-        b = dbank(t)
-        act(rbank(t), 0, B, T[b][:, 0:B], [b], AF.Relu, -1.0, 16.0)
+    def moves1_w():
+        for bank, idn, o in (("b7", "NID", B), ("b5", "IDN", 0)):
+            mm(bank, T[bank][:, 0:B], idn, 0, T.SR1[:, o:o + B], [("SR1", o, o + B)], True, False)
 
-    def left_relu(t):
-        act("DX", K * t, K * t + B, T.TM[:, B * (t - 1):B * t], [("TM", B * (t - 1), B * t)], AF.Relu)
+    def moves1_x(i):
+        bank = ("b7", "b5")[i]
+        mm(bank, T[bank][:, 0:B], "WN", 0, T.G1[:, 0:B], [("G1", 0, B)], False, False)
+        mm(bank, T[bank][:, 0:B], "WP", 0, T.G1[:, B:K], [("G1", B, K)], False, True)
 
-    def right_min(r, t):
-        b, sr, o = rbank(t), "SR%d" % r, K * (t - 1)
-        tt("DX", K * t + B, K * t + K, T[b][:, 0:B], T[sr][:, o:o + B], [b, (sr, o, o + B)], A.min)
+    def moves1_y():
+        act("UB", 0, B, T.b7[:, 0:B], ["b7"], AF.Relu, -1.0)
+        act("UB", B, K, T.b5[:, 0:B], ["b5"], AF.Relu, 1.0, -16.0)
+
+    def moves1_z():
+        for i, bank, o in ((0, "b7", B), (1, "b5", 0)):
+            mm(bank, T[bank][:, 0:B], "IDN", 0, T.SR1[:, o:o + B], [("SR1", o, o + B)], True, False)
+            mm(bank, T[bank][:, 0:B], "NID", 0, T.UB[:, B * i:B * i + B], [("UB", B * i, B * i + B)], False, True)
+            act("DX", K + B * i, K + B * i + B, T[bank][:, 0:B], [bank], AF.Relu)
+
+    def relus(t):
+        b, rb = dbank(t), rbank(t)
+        act(rb, 0, B, T[b][:, 0:B], [b], AF.Relu, -1.0, 16.0)
+        act(b, 0, B, T[b][:, 0:B], [b], AF.Relu)
+
+    def mins(r, t):
+        sr, o = "SR%d" % r, K * (t - 1)
+        for i, b in ((1, rbank(t)), (0, dbank(t))):
+            c = o + B - B * i
+            tt("DX", K * t + B * i, K * t + B * i + B, T[b][:, 0:B], T[sr][:, c:c + B], [b, (sr, c, c + B)], A.min)
 
     def down(r):
-        tab, pt, h, wb, rm = ["%s%d" % (n, r) for n in ("TAB", "PT", "H", "WB", "RM")]
+        tab = "TAB"
+        pt, h, wb, rm = ["%s%d" % (n, r) for n in ("PT", "H", "WB", "RM")]
         for i in (1, 0):
             d = K * 3 + B * i
             tt(tab, EDGE + B * i, EDGE + B * i + B, T.b6[:, 0:B], T.DX[:, d:d + B], ["b6", ("DX", d, d + B)], A.add)
@@ -346,101 +370,88 @@ def rank_program(g, core, T, topo):
 
     dma("y", [], [("KI", 0, 192)], T.KI[:, 0:192], T.kids[:, 0:192])
     dma("s", [], [("H0", 0, L)], T.H0[:, 0:L], T.x[:, :])
-    dma("y", [], ["MLI"], T.MLI[:, :], T.ml[:, :])
-    dma("y", [], ["MRI"], T.MRI[:, :], T.mr[:, :])
+    dma("y", [], [("MI", 0, 128)], T.MI[:, 0:128], T.ml[:, :])
+    dma("y", [], [("MI", 128, 256)], T.MI[:, 128:256], T.mr[:, :])
     dma("y", [], ["WI"], T.WI[:, :], T.w[:, :])
     dma("y", [], [("KI", 192, 384)], T.KI[:, 192:384], T.kids[:, 192:384])
 
     def val(t):
         iota("VAL", K * t, K * t + K, [[1, K]], EDGE + K * (3 - t), 0)
 
-    fill("ONES", 0, 1280, 1.0)
-    for i in range(2):
-        act("PW0", 1536 + 1280 * i, 2816 + 1280 * i, T.ONES[:, 0:1280], [("ONES", 0, 1280)], AF.Copy, 0.0)
-    fill("PW0", 0, 1536, 0.0)
+    fill("ZZ", 0, 256, 0.0)
+    for r in range(RO):
+        dma("sy"[r], ["ZZ"], ["PW%d" % r], T["PW%d" % r][0:128:16, :], T.ZZ[:, :])
+    fill("SZ", 0, L, 1.0)
+    act("TAB", 0, 16, T.SZ[:, 0:16], [("SZ", 0, 16)], AF.Silu, 0.0)
     val(0)
-    select("BLA", "ONES", 128, [[-16, 8], [0, 16]], A.is_ge, 0, 1)
+    select("BLA", "SZ", 128, [[-16, 8], [0, 16]], A.is_ge, 0, 1)
     select("BLK", "BLA", 128, [[16, 8], [0, 16]], A.is_ge, 15, -1)
     val(1)
-    select("IDN", "ONES", 128, [[-1, 128]], A.is_equal, 0, 1)
+    select("IDN", "SZ", 128, [[-1, 128]], A.is_equal, 0, 1)
     val(2)
     val(3)
-    lists(0)
-    scat(0, 0)
-    fill("SZ0", 0, L, 1.0)
-    fill("SZ0", L, L + B, 2.0)
-    fill("CB", 0, 128, -0.375 / 128)
-    ts("ML", 0, 128, T.MLI[:, :], ["MLI"], 0.25, None, A.mult)
-    ts("MR", 0, 128, T.MRI[:, :], ["MRI"], 0.25, None, A.mult)
+    select("DQ", "SZ", 2048, [[-1024, 16], [-16, 8], [1023, 16]], A.is_equal, 0, 1)
     select("TRI", "BLK", 128, [[-1, 128]], A.is_ge, 0, 1)
-    iota("PI", 0, 8, [[0, 8]], 0, 1, False)
-    iota("CI", 0, 72, [[1, 72]], SLOT, 0)
-
-    scat(0, 1)
-    scat(0, 2)
-    scat(0, 3)
-    conv(0)
-    bias(0)
-    bias(1)
-    gather(0, 0, 0, "v")
-    gather(0, 0, 1, "v")
-    sums(0)
+    iota("C72", 0, 16, [[0, 16]], 72, 0)
+    iota("CI", 0, 72, [[1, 72]], SLOT + 16 * 72, 0)
+    select("EQ", "SZ", 2048, [[-1, 16], [-16, 8], [0, 16]], A.is_equal, 0, 1)
+    fill("SZ", L, L + B, 2.0)
+    fill("CB", 0, 128, -0.375 / 128)
+    lists(0)
+    ts("MM", 0, 256, T.MI[:, :], ["MI"], 0.25, None, A.mult)
     ts("WP", 0, 128, T.BLK[:, :], ["BLK", "WI"], T.WI[:, 0:1], 16.0, A.mult, A.mult)
     ts("WN", 0, 128, T.BLK[:, :], ["BLK", "WI"], T.WI[:, 0:1], -16.0, A.mult, A.mult)
-    fill("ONES", 1280, 2048, 1.0)
-    select("EQ", "ONES", 2048, [[-1, 16], [-16, 8], [0, 16]], A.is_equal, 0, 1)
-    select("DQ", "EQ", 2048, [[1, 16], [0, 8], [-1, 16]], A.is_equal, 0, 0)
-    iota("PW1", 0, 4096, [[0, 4096]], 0, 0)
+    lists(1)
+
+    for t in range(4):
+        scat(0, t)
+    conv(0)
+
+    def up0(t, q):
+        for h in range(2):
+            gather(0, t, 0, h, q)
+            gather(0, t, 1, h, q)
+        if t < 3:
+            sums(t)
+
+    bias()
+    up0(0, "v")
     diff(0)
     vectors(0, 0)
+    bias()
     size_gather(0, 1, "v")
     size_add(0, 1)
-    gather(0, 1, 0, "v")
-    gather(0, 1, 1, "v")
-    sums(1)
+    up0(1, "v")
     size_store(0, 1, "v")
-    moves0()
     diff(1)
-    bias(2)
     vectors(0, 1)
+    bias()
     size_gather(0, 2, "v")
     size_add(0, 2)
-    gather(0, 2, 0, "v")
-    gather(0, 2, 1, "v")
-    sums(2)
+    relus(1)
+    up0(2, "v")
     size_store(0, 2, "v")
     diff(2)
-    size_gather(0, 3, "s")
-    size_add(0, 3)
-    ts("QI", 0, 8, T.PI[:, :], ["PI"], 15, None, A.bitwise_and)
-    fill("ZF", 0, 224, 0.0)
     vectors(0, 2)
-    right_relu(1)
-    size_store(0, 3, "s")
+    mm("b6", T.b6[:, 0:16], "TRI", 0, T.C72[:, :], ["C72"], True, True)
+    size_gather(0, 3, "v")
+    size_add(0, 3)
+    op("v", ["CI", "b6"], ["CT"], lambda: V.tensor_scalar(T.CT[:, :], T.CI[:, :], T.b6[:, 0:1], None, A.subtract))
+    mins(0, 1)
+    size_store(0, 3, "v")
+    relus(2)
+    mins(0, 2)
+    up0(3, "s")
     size_list(0)
-    gather(0, 3, 0, "v")
-    gather(0, 3, 1, "v")
-    vcopy("QF", 0, 8, T.QI[:, :], ["QI"])
-    fill("TAB0", 0, 16, 0.0)
-    ts("Q72", 0, 8, T.QF[:, :], ["QF"], 72.0, None, A.mult)
-    fill("TAB1", 0, 16, 0.0)
-    ts("CT", 0, 72, T.CI[:, :], ["CI", "Q72"], T.Q72[:, 0:1], None, A.add)
-    left_min(0, 1)
-    left_relu(1)
-    right_min(0, 1)
-    left_min(0, 2)
-    right_relu(2)
-    left_relu(2)
-    root_sizes(0)
-    right_min(0, 2)
     diff(3)
+    root_flags(0)
+    relus(3)
+    moves0_a()
+    root_sizes(0)
     root_starts(0)
-    left_min(0, 3)
-    right_relu(3)
-    left_relu(3)
-    right_min(0, 3)
-    root_rows3(0)
-    root_rows(0, lambda: (lists(1), fill("SZ1", 0, L, 1.0), fill("SZ1", L, L + B, 2.0)))
+    mins(0, 3)
+    moves0_b()
+    root_rows(0, "sss")
     root_leaves(0)
     size_gather(1, 1, "s")
     scat(1, 0)
@@ -459,40 +470,41 @@ def rank_program(g, core, T, topo):
     size_store(1, 3, "s")
     exchange(0)
     size_list(1)
+    root_flags(1)
     root_sizes(1)
     root_starts(1)
-    bias(0)
-    bias(1)
-    root_rows3(1)
-    root_rows(1, None)
+    bias()
+    root_rows(1, "svs")
     root_leaves(1)
+    act("NID", 0, 128, T.IDN[:, :], ["IDN"], AF.Copy, -1.0)
+    moves1_w()
 
     for t in range(NT):
-        gather(1, t, 0, "v")
-        gather(1, t, 1, "s")
+        for h in range(2):
+            gather(1, t, 0, h, "v")
+            gather(1, t, 1, h, "s")
         if t < 3:
             sums(t)
         if t == 1:
-            moves0()
+            moves0_a()
+            moves1_x(0)
+        else:
+            diff(t)
         if t == 2:
-            left_min(1, 1)
-            right_relu(1)
-            left_relu(1)
-        if t == 3:
-            right_relu(2)
-            right_min(1, 1)
-            left_min(1, 2)
-        diff(t)
-        if t == 1:
-            bias(2)
+            moves0_b()
+            moves1_x(1)
         if t < 3:
             vectors(1, t)
-    right_min(1, 2)
-    right_relu(3)
-    left_min(1, 3)
-    left_relu(3)
-    left_relu(2)
-    right_min(1, 3)
+        if t < 2:
+            bias()
+    tt("UX", 0, B, T.b4[:, 0:B], T.SR1[:, K + B:K + K], ["b4", ("SR1", K + B, K + K)], A.min)
+    act("b1", 0, B, T.b4[:, 0:B], ["b4"], AF.Relu, -1.0, 16.0)
+    tt("DX", 2 * K + B, 3 * K, T.b1[:, 0:B], T.SR1[:, K:K + B], ["b1", ("SR1", K, K + B)], A.min)
+    relus(3)
+    mins(1, 3)
+    act("DX", 2 * K, 2 * K + B, T.UX[:, 0:B], [("UX", 0, B)], AF.Relu)
+    moves1_y()
+    moves1_z()
     down(1)
     exchange(1)
     dma("s", [("WB1", 512 * me, 512 * me + 512)], [], T.y[:, 512 * me:512 * me + 512], T.WB1[:, 512 * me:512 * me + 512])

from concourse.bass import DstId, RemoteDMATransfer
from concourse.mybir import dt, AluOpType, ActivationFunctionType

A = AluOpType
AF = ActivationFunctionType
L, NT, B, RO = 2048, 4, 384, 2
K = 2 * B
C = B // 2
SLOT = 16
EDGE = SLOT + 16 * 72
TW = EDGE + NT * K
MAGIC = 12582912.0
PART = ((0, 64), (64, 128))

SCRATCH = {
    "KI": ("sbuf", [128, 384], "int32"), "K16": ("sbuf", [128, 384], "uint16"),
    "ZA": ("sbuf", [128, 384], "int32"), "ZB": ("sbuf", [128, 384], "int32"), "SG": ("sbuf", [128, 384], "uint16"),
    "VAL": ("sbuf", [128, NT * K], "float32"), "ZZ": ("sbuf", [128, 256], "float32"),
    "SZ": ("sbuf", [128, L + NT * B], "bfloat16"), "TAB": ("sbuf", [128, TW], "float32"),
    "IDN": ("sbuf", [128, 128], "bfloat16"), "NID": ("sbuf", [128, 128], "bfloat16"),
    "BLA": ("sbuf", [128, 128], "bfloat16"), "BLK": ("sbuf", [128, 128], "bfloat16"), "TRI": ("sbuf", [128, 128], "bfloat16"),
    "EQ": ("sbuf", [128, 2048], "bfloat16"), "DQ": ("sbuf", [128, 2048], "bfloat16"),
    "C72": ("sbuf", [128, 16], "bfloat16"), "CI": ("sbuf", [128, 72], "float32"), "CT": ("sbuf", [128, 72], "float32"),
    "CB": ("sbuf", [128, 128], "bfloat16"),
    "MI": ("sbuf", [128, 256], "bfloat16"), "WI": ("sbuf", [128, 1], "bfloat16"), "MM": ("sbuf", [128, 256], "bfloat16"),
    "WP": ("sbuf", [128, 128], "bfloat16"), "WN": ("sbuf", [128, 128], "bfloat16"),
    "F16": ("sbuf", [128, B], "float16"), "DX": ("sbuf", [128, NT * K], "float32"),
    "UX": ("sbuf", [128, B], "float32"), "UB": ("sbuf", [128, K], "bfloat16"),
    "PR": ("sbuf", [128, 2048], "float16"), "QA": ("sbuf", [128, 128], "int32"), "QB": ("sbuf", [128, 128], "int32"),
    "QL": ("sbuf", [128, 128], "uint16"),
    "YL": ("sbuf", [128, L], "bfloat16"),
}
for _t in range(NT):
    SCRATCH["G%d" % _t] = ("sbuf", [128, K], "bfloat16")
for _r in range(RO):
    SCRATCH.update({
        "H%d" % _r: ("sbuf", [128, L + 3 * B], "bfloat16"),
        "PW%d" % _r: ("sbuf", [128, 4096], "float32"), "PL%d" % _r: ("sbuf", [128, 256], "float32"),
        "NA%d" % _r: ("sbuf", [128, 72], "float32"), "PT%d" % _r: ("sbuf", [128, 200], "uint16"),
        "RS%d" % _r: ("sbuf", [128, 224], "bfloat16"), "INC%d" % _r: ("sbuf", [128, 224], "float32"),
        "RL%d" % _r: ("sbuf", [128, 224], "float16"), "RM%d" % _r: ("sbuf", [128, 128], "float16"),
        "SR%d" % _r: ("sbuf", [128, 3 * K], "bfloat16"), "WB%d" % _r: ("sbuf", [128, L], "bfloat16"),
    })
for _b in range(8):
    SCRATCH["b%d" % _b] = ("psum", [128, 512], "float32")
PSUM = ["b%d" % i for i in range(8)]

SEMAPHORES = ["qv", "qs", "qp", "qg", "sent", "arr0"] + ["arr1_%d" % i for i in range(4)] + ["d%d" % i for i in range(16)]


def rank_program(g, core, T, topo):
    me = T.rank_of(core)
    if me is None:
        return
    cores = list(T.cores)
    eng = {"v": g.vector, "s": g.scalar, "p": g.tensor, "g": g, "y": g.sync}
    known = {q: {} for q in eng}
    total = {}
    acc = {}
    ndma = [0]

    def span(x):
        if isinstance(x, str):
            return x, 0, SCRATCH[x][1][1]
        return x

    def learn(q, sem, n, snap):
        k = known[q]
        if k.get(sem, 0) < n:
            k[sem] = n
        for s2, n2 in snap.items():
            if k.get(s2, 0) < n2:
                k[s2] = n2

    def sync_for(q, reads, writes):
        need = {}
        for kind, lst in (("r", reads), ("w", writes)):
            for x in lst:
                b, lo, hi = span(x)
                ps = b in PSUM
                for rk, rlo, rhi, rq, sem, n, snap in acc.get(b, []):
                    if ps:
                        if rq == q and (q == "p" or (kind == "r" and rk == "r")):
                            continue
                    elif rhi <= lo or rlo >= hi or (kind == "r" and rk == "r"):
                        continue
                    if known[q].get(sem, 0) >= n:
                        continue
                    if sem not in need or need[sem][0] < n:
                        need[sem] = (n, snap)
        for sem in sorted(need, key=lambda s: -len(need[s][1])):
            n, snap = need[sem]
            if known[q].get(sem, 0) < n:
                eng[q].wait_ge(T.sem[sem], n)
                learn(q, sem, n, snap)

    def note(q, reads, writes, sem, n):
        snap = dict(known[q])
        for kind, lst in (("r", reads), ("w", writes)):
            for x in lst:
                b, lo, hi = span(x)
                old = acc.setdefault(b, [])
                if kind == "w" and b not in PSUM:
                    old[:] = [o for o in old if not (o[1] >= lo and o[2] <= hi)]
                old.append((kind, lo, hi, q, sem, n, snap))

    def op(q, reads, writes, call):
        sync_for(q, reads, writes)
        sem = "q" + q
        total[sem] = total.get(sem, 0) + 1
        call().then_inc(T.sem[sem], 1)
        note(q, reads, writes, sem, total[sem])

    def dma(q, reads, writes, out, in_):
        sync_for(q, reads, writes)
        sem = "d%d" % ndma[0]
        ndma[0] += 1
        total[sem] = 16
        eng[q].dma_start(out=out, in_=in_).then_inc(T.sem[sem], 16)
        note(q, reads, writes, sem, 16)

    V, S, P = g.vector, g.scalar, g.tensor

    def ts(b_out, lo, hi, in_ap, reads, s1, s2, o0, o1=None):
        o = T[b_out][:, lo:hi]
        if o1 is None:
            op("v", reads, [(b_out, lo, hi)], lambda: V.tensor_scalar(o, in_ap, s1, None, o0))
        else:
            op("v", reads, [(b_out, lo, hi)], lambda: V.tensor_scalar(o, in_ap, s1, s2, o0, o1))

    def tt(b_out, lo, hi, a0, a1, reads, o0):
        op("v", reads, [(b_out, lo, hi)], lambda: V.tensor_tensor(T[b_out][:, lo:hi], a0, a1, o0))

    def vcopy(b_out, lo, hi, in_ap, reads):
        op("v", reads, [(b_out, lo, hi)], lambda: V.tensor_copy(T[b_out][:, lo:hi], in_ap))

    def fill(b, lo, hi, c):
        op("v", [], [(b, lo, hi)], lambda: V.memset(T[b][:, lo:hi], c))

    def act(b_out, lo, hi, in_ap, reads, func, scale=None, bias=None):
        o = T[b_out][:, lo:hi]
        if bias is not None:
            op("s", reads, [(b_out, lo, hi)], lambda: S.activation(o, in_ap, func, bias=bias, scale=scale))
        elif scale is None:
            op("s", reads, [(b_out, lo, hi)], lambda: S.activation(o, in_ap, func))
        else:
            op("s", reads, [(b_out, lo, hi)], lambda: S.activation(o, in_ap, func, scale=scale))

    def copy(q, b_out, lo, hi, in_ap, reads):
        if q == "v":
            vcopy(b_out, lo, hi, in_ap, reads)
        else:
            act(b_out, lo, hi, in_ap, reads, AF.Copy)

    def mm(bank, out_ap, lhs, lo, rhs_ap, reads, start, stop):
        op("p", [(lhs, lo, lo + 128)] + reads, [bank], lambda: P.matmul(out_ap, T[lhs][:, lo:lo + 128], rhs_ap, start, stop))

    def iota(b, lo, hi, pattern, base, cm, flag=True):
        if flag:
            op("g", [], [(b, lo, hi)], lambda: g.iota(T[b][:, lo:hi], pattern, base, cm, allow_small_or_imprecise_dtypes=True))
        else:
            op("g", [], [(b, lo, hi)], lambda: g.iota(T[b][:, lo:hi], pattern, base, cm))

    def select(b_out, b_in, n, pattern, cmp, base, cm):
        op("g", [(b_in, 0, n)], [(b_out, 0, n)], lambda: g.affine_select(T[b_out][:, 0:n], T[b_in][:, 0:n], pattern, cmp, 0.0, base, cm))

    def lists(r):
        lo, hi = 192 * r, 192 * r + 192
        ki = T.KI[:, lo:hi]
        ts("ZA", lo, hi, ki, [("KI", lo, hi)], 4097, None, A.mult)
        vcopy("K16", lo, hi, ki, [("KI", lo, hi)])
        ts("ZB", lo, hi, T.ZA[:, lo:hi], [("ZA", lo, hi)], 4, 4095, A.arith_shift_right, A.bitwise_and)
        vcopy("SG", lo, hi, T.ZB[:, lo:hi], [("ZB", lo, hi)])

    def scat(r, t):
        b, c = "PW%d" % r, 192 * r + 48 * t
        op("s", [("SG", c, c + 48), ("VAL", K * t, K * t + K)], [b],
           lambda: S.activation(T[b][:, :].indirect(T.SG[:, c:c + 48]), T.VAL[:, K * t:K * t + K], AF.Silu))

    def conv(r):
        b, o = "PW%d" % r, "PL%d" % r
        dma("y", [b], [o], T[o][:, :], T[b][0:128:16, :])

    def size_gather(r, t, q):
        w, c, lo = L + B * t, 192 * r + 48 * t, K * (t - 1)
        copy(q, "SR%d" % r, lo, lo + K, T.SZ[:, 0:w].indirect(T.K16[:, c:c + 48]), [("SZ", 0, w), ("K16", c, c + 48)])

    def size_add(r, t):
        sr, lo = "SR%d" % r, K * (t - 1)
        for i in range(2):
            c = lo + B * i
            mm("b5", T.b5[:, 0:B], "IDN", 0, T[sr][:, c:c + B], [(sr, c, c + B)], i == 0, i == 1)

    def size_store(r, t, q):
        copy(q, "SZ", L + B * t, L + B * t + B, T.b5[:, 0:B], ["b5"])

    def size_list(r):
        for q in range(16):
            mm("b6", T.b6[:, 0:96], "DQ", 128 * q, T.SZ[:, L + q:L + 4 * B:16], [("SZ", L, L + 4 * B)], q == 0, q == 15)

    def root_flags(r):
        pl, rs = "PL%d" % r, "RS%d" % r
        act(rs, 0, 224, T[pl][:, 0:224], [pl], AF.Relu, -1.0, 1.0)

    def root_sizes(r):
        rs, na = "RS%d" % r, "NA%d" % r
        tt(na, 0, 72, T[rs][:, 128:200], T.CT[:, :], [(rs, 128, 200), "CT"], A.mult)
        tt(rs, 128, 224, T[rs][:, 128:224], T.b6[:, 0:96], [(rs, 128, 224), "b6"], A.mult)

    def root_starts(r):
        pl, rs, na, pt, inc, rl = ["%s%d" % (n, r) for n in ("PL", "RS", "NA", "PT", "INC", "RL")]
        mm("b6", T.b6[:, 224:448], "BLK", 0, T[rs][:, :], [rs], True, True)
        mm("b6", T.b6[:, 0:224], "TRI", 0, T[rs][:, :], [rs], True, True)
        tt(pl, 128, 200, T[na][:, :], T[pl][:, 128:200], [na, (pl, 128, 200)], A.add)
        op("v", ["b6", rs], [inc], lambda: V.tensor_tensor_scan(T[inc][:, :], T.b6[:, 224:448], T[rs][:, :], 0.0, A.add, A.max))
        tt(rl, 0, 224, T[inc][:, :], T.b6[:, 0:224], [inc, "b6"], A.subtract)
        ts(pt, 0, 200, T[pl][:, 0:200], [pl], 0.25, None, A.add)

    def root_rows3(r):
        rl = "RL%d" % r
        for q in range(16):
            mm("b6", T.b6[:, q:B:16], "EQ", 128 * q, T[rl][:, 200:224], [(rl, 200, 224)], True, True)

    def root_rows(r, es):
        rl = "RL%d" % r
        for bank, qs, e in (("b5", range(0, 6), es[0]), ("b4", range(6, 12), es[1]), ("b2", range(12, 16), es[2])):
            for i, q in enumerate(qs):
                mm(bank, T[bank][:, 72 * i:72 * i + 72], "EQ", 128 * q, T[rl][:, 128:200], [(rl, 128, 200)], True, True)
            c = SLOT + 72 * qs[0]
            copy(e, "TAB", c, c + 72 * len(qs), T[bank][:, 0:72 * len(qs)], [bank])
            if bank == "b5":
                root_rows3(r)

    def root_leaves(r):
        rl, rs = "RL%d" % r, "RS%d" % r
        tt("RM%d" % r, 0, 128, T[rl][:, 0:128], T[rs][:, 0:128], [(rl, 0, 128), (rs, 0, 128)], A.mult)

    def bias():
        for b in ("b0", "b1"):
            mm(b, T[b][:, 0:C], "CB", 0, T.SZ[:, 0:C], [("SZ", 0, C)], True, False)

    def gather(r, t, side, h, q):
        hb, w, c, o = "H%d" % r, L + B * t, 192 * r + 48 * t + 24 * side + 12 * h, B * side + C * h
        copy(q, "G%d" % t, o, o + C, T[hb][:, 0:w].indirect(T.K16[:, c:c + 12]), [(hb, 0, w), ("K16", c, c + 12)])

    def sums(t):
        gb = "G%d" % t
        for h, b in enumerate(("b0", "b1")):
            for side in range(2):
                o = B * side + C * h
                mm(b, T[b][:, 0:C], "MM", 128 * side, T[gb][:, o:o + C], [(gb, o, o + C)], False, side == 1)

    def dbank(t):
        return ("b2", "b7", "b4", "b0")[t]

    def rbank(t):
        return ("b3", "b3", "b1", "b3")[t]

    def diff(t):
        b, gb = dbank(t), "G%d" % t
        mm(b, T[b][:, 0:B], "WN", 0, T[gb][:, 0:B], [(gb, 0, B)], True, False)
        mm(b, T[b][:, 0:B], "WP", 0, T[gb][:, B:K], [(gb, B, K)], False, True)

    def vectors(r, t):
        for h, b in enumerate(("b0", "b1")):
            ts("F16", C * h, C * h + C, T[b][:, 0:C], [b], -127.0, 127.0, A.max, A.min)
        for h in range(2):
            lo = L + B * t + C * h
            ts("H%d" % r, lo, lo + C, T.F16[:, C * h:C * h + C], [("F16", C * h, C * h + C)], MAGIC, MAGIC, A.add, A.subtract)

    def moves0_a():
        act("UX", 0, B, T.b2[:, 0:B], ["b2"], AF.Relu, -1.0, 1.0)

    def moves0_b():
        act("DX", 0, B, T.UX[:, 0:B], [("UX", 0, B)], AF.Relu, -1.0, 1.0)
        act("DX", B, K, T.DX[:, 0:B], [("DX", 0, B)], AF.Relu, -1.0, 1.0)

    def moves1_w():
        for bank, idn, o in (("b7", "NID", B), ("b5", "IDN", 0)):
            mm(bank, T[bank][:, 0:B], idn, 0, T.SR1[:, o:o + B], [("SR1", o, o + B)], True, False)

    def moves1_x(i):
        bank = ("b7", "b5")[i]
        mm(bank, T[bank][:, 0:B], "WN", 0, T.G1[:, 0:B], [("G1", 0, B)], False, False)
        mm(bank, T[bank][:, 0:B], "WP", 0, T.G1[:, B:K], [("G1", B, K)], False, True)

    def moves1_y():
        act("UB", 0, B, T.b7[:, 0:B], ["b7"], AF.Relu, -1.0)
        act("UB", B, K, T.b5[:, 0:B], ["b5"], AF.Relu, 1.0, -16.0)

    def moves1_z():
        for i, bank, o in ((0, "b7", B), (1, "b5", 0)):
            mm(bank, T[bank][:, 0:B], "IDN", 0, T.SR1[:, o:o + B], [("SR1", o, o + B)], True, False)
            mm(bank, T[bank][:, 0:B], "NID", 0, T.UB[:, B * i:B * i + B], [("UB", B * i, B * i + B)], False, True)
            act("DX", K + B * i, K + B * i + B, T[bank][:, 0:B], [bank], AF.Relu)

    def relus(t):
        b, rb = dbank(t), rbank(t)
        act(rb, 0, B, T[b][:, 0:B], [b], AF.Relu, -1.0, 16.0)
        act(b, 0, B, T[b][:, 0:B], [b], AF.Relu)

    def mins(r, t):
        sr, o = "SR%d" % r, K * (t - 1)
        for i, b in ((1, rbank(t)), (0, dbank(t))):
            c = o + B - B * i
            tt("DX", K * t + B * i, K * t + B * i + B, T[b][:, 0:B], T[sr][:, c:c + B], [b, (sr, c, c + B)], A.min)

    def down(r):
        tab = "TAB"
        pt, h, wb, rm = ["%s%d" % (n, r) for n in ("PT", "H", "WB", "RM")]
        for i in (1, 0):
            d = K * 3 + B * i
            tt(tab, EDGE + B * i, EDGE + B * i + B, T.b6[:, 0:B], T.DX[:, d:d + B], ["b6", ("DX", d, d + B)], A.add)
        for t in (2, 1, 0):
            w = EDGE + K * (3 - t)
            c = 128 + 24 * t
            for i in range(2):
                d = K * t + B * i
                tt(tab, w + B * i, w + B * i + B, T[tab][:, 0:w].indirect(T[pt][:, c:c + 24]), T.DX[:, d:d + B],
                   [(tab, 0, w), (pt, c, c + 24), ("DX", d, d + B)], A.add)
        for k, (lo, hi) in enumerate(PART):
            vcopy("PR", 16 * lo, 16 * hi, T[tab][:, :].indirect(T[pt][:, lo:hi]), [tab, (pt, lo, hi)])
            b = "b%d" % (4 + k)
            mm(b, T[b][:, 0:hi - lo], "IDN", 0, T[rm][:, lo:hi], [(rm, lo, hi)], True, False)
            for q in range(16):
                mm(b, T[b][:, 0:hi - lo], "DQ", 128 * q, T.PR[:, 16 * lo + q:16 * hi:16], [("PR", 16 * lo, 16 * hi)], False, q == 15)
        for k, (lo, hi) in enumerate(PART):
            b = "b%d" % (4 + k)
            ts("QA", lo, hi, T[b][:, 0:hi - lo], [b], 2049.0, None, A.mult)
            ts("QB", lo, hi, T.QA[:, lo:hi], [("QA", lo, hi)], 2, 2047, A.arith_shift_right, A.bitwise_and)
            vcopy("QL", lo, hi, T.QB[:, lo:hi], [("QB", lo, hi)])
            op("v", [("QL", lo, hi), (h, 16 * lo, 16 * hi)], [wb],
               lambda: V.tensor_copy(T[wb][:, :].indirect(T.QL[:, lo:hi]), T[h][:, 16 * lo:16 * hi]))

    def plan(src):
        s = cores[src]
        off = [d for d in range(4) if d != src and topo.chip(cores[d]) != topo.chip(s)]
        on = [d for d in range(4) if d != src and topo.chip(cores[d]) == topo.chip(s)]
        oe = topo.engines(s, cores[off[0]])
        n = len(oe) // len(off)
        res = {d: oe[n * i:n * i + n] for i, d in enumerate(off)}
        for d in on:
            res[d] = [e for e in topo.engines(s, cores[d]) if e not in oe]
        return res

    def exchange(r):
        wb = "WB%d" % r
        dst = ("H1", "YL")[r]
        sem = "arr0" if r == 0 else "arr1_%d" % me
        tr = []
        n = 0
        for d, es in plan(me).items():
            rid, pid, _se = topo.addr(cores[d])
            m = sum(1 << e for e in es)
            n += len(es)
            tr.append(RemoteDMATransfer(dst_ids=[DstId(rid=rid, pnc=pid)], dma_engine_mask=m, remote_sem=T.sem[sem],
                                        src=T[wb][:, 512 * d:512 * d + 512], dst=T[dst][:, 512 * me:512 * me + 512]))
        sync_for("g", [wb], [])
        g.remote_dma_fused(tr, local_sem=T.sem["sent"])
        total["sent"] = total.get("sent", 0) + n
        note("g", [wb], [], "sent", total["sent"])
        others = [s for s in range(4) if s != me]
        got = sum(len(plan(s)[me]) for s in others)
        for s in others:
            sem, n = ("arr0", got) if r == 0 else ("arr1_%d" % s, len(plan(s)[me]))
            total[sem] = n
            acc.setdefault(dst, []).append(("w", 512 * s, 512 * s + 512, "x", sem, n, {}))
        if r == 0:
            vcopy(dst, 512 * me, 512 * me + 512, T[wb][:, 512 * me:512 * me + 512], [wb])

    dma("y", [], [("KI", 0, 192)], T.KI[:, 0:192], T.kids[:, 0:192])
    dma("s", [], [("H0", 0, L)], T.H0[:, 0:L], T.x[:, :])
    dma("y", [], [("MI", 0, 128)], T.MI[:, 0:128], T.ml[:, :])
    dma("y", [], [("MI", 128, 256)], T.MI[:, 128:256], T.mr[:, :])
    dma("y", [], ["WI"], T.WI[:, :], T.w[:, :])
    dma("y", [], [("KI", 192, 384)], T.KI[:, 192:384], T.kids[:, 192:384])

    def val(t):
        iota("VAL", K * t, K * t + K, [[1, K]], EDGE + K * (3 - t), 0)

    fill("ZZ", 0, 256, 0.0)
    for r in range(RO):
        dma("sy"[r], ["ZZ"], ["PW%d" % r], T["PW%d" % r][0:128:16, :], T.ZZ[:, :])
    fill("SZ", 0, L, 1.0)
    act("TAB", 0, 16, T.SZ[:, 0:16], [("SZ", 0, 16)], AF.Silu, 0.0)
    val(0)
    select("BLA", "SZ", 128, [[-16, 8], [0, 16]], A.is_ge, 0, 1)
    select("BLK", "BLA", 128, [[16, 8], [0, 16]], A.is_ge, 15, -1)
    val(1)
    select("IDN", "SZ", 128, [[-1, 128]], A.is_equal, 0, 1)
    val(2)
    val(3)
    select("DQ", "SZ", 2048, [[-1024, 16], [-16, 8], [1023, 16]], A.is_equal, 0, 1)
    select("TRI", "BLK", 128, [[-1, 128]], A.is_ge, 0, 1)
    iota("C72", 0, 16, [[0, 16]], 72, 0)
    iota("CI", 0, 72, [[1, 72]], SLOT + 16 * 72, 0)
    select("EQ", "SZ", 2048, [[-1, 16], [-16, 8], [0, 16]], A.is_equal, 0, 1)
    fill("SZ", L, L + B, 2.0)
    fill("CB", 0, 128, -0.375 / 128)
    lists(0)
    ts("MM", 0, 256, T.MI[:, :], ["MI"], 0.25, None, A.mult)
    ts("WP", 0, 128, T.BLK[:, :], ["BLK", "WI"], T.WI[:, 0:1], 16.0, A.mult, A.mult)
    ts("WN", 0, 128, T.BLK[:, :], ["BLK", "WI"], T.WI[:, 0:1], -16.0, A.mult, A.mult)
    lists(1)

    for t in range(4):
        scat(0, t)
    conv(0)

    def up0(t, q):
        for h in range(2):
            gather(0, t, 0, h, q)
            gather(0, t, 1, h, q)
        if t < 3:
            sums(t)

    bias()
    up0(0, "v")
    diff(0)
    vectors(0, 0)
    bias()
    size_gather(0, 1, "v")
    size_add(0, 1)
    up0(1, "v")
    size_store(0, 1, "v")
    diff(1)
    vectors(0, 1)
    bias()
    size_gather(0, 2, "v")
    size_add(0, 2)
    relus(1)
    up0(2, "v")
    size_store(0, 2, "v")
    diff(2)
    vectors(0, 2)
    mm("b6", T.b6[:, 0:16], "TRI", 0, T.C72[:, :], ["C72"], True, True)
    size_gather(0, 3, "v")
    size_add(0, 3)
    op("v", ["CI", "b6"], ["CT"], lambda: V.tensor_scalar(T.CT[:, :], T.CI[:, :], T.b6[:, 0:1], None, A.subtract))
    mins(0, 1)
    size_store(0, 3, "v")
    relus(2)
    mins(0, 2)
    up0(3, "s")
    size_list(0)
    diff(3)
    root_flags(0)
    relus(3)
    moves0_a()
    root_sizes(0)
    root_starts(0)
    mins(0, 3)
    moves0_b()
    root_rows(0, "sss")
    root_leaves(0)
    size_gather(1, 1, "s")
    scat(1, 0)
    size_add(1, 1)
    size_store(1, 1, "s")
    size_gather(1, 2, "s")
    scat(1, 1)
    scat(1, 2)
    scat(1, 3)
    conv(1)
    down(0)
    size_add(1, 2)
    size_store(1, 2, "s")
    size_gather(1, 3, "s")
    size_add(1, 3)
    size_store(1, 3, "s")
    exchange(0)
    size_list(1)
    root_flags(1)
    root_sizes(1)
    root_starts(1)
    bias()
    root_rows(1, "svs")
    root_leaves(1)
    act("NID", 0, 128, T.IDN[:, :], ["IDN"], AF.Copy, -1.0)
    moves1_w()

    for t in range(NT):
        for h in range(2):
            gather(1, t, 0, h, "v")
            gather(1, t, 1, h, "s")
        if t < 3:
            sums(t)
        if t == 1:
            moves0_a()
            moves1_x(0)
        else:
            diff(t)
        if t == 2:
            moves0_b()
            moves1_x(1)
        if t < 3:
            vectors(1, t)
        if t < 2:
            bias()
    tt("UX", 0, B, T.b4[:, 0:B], T.SR1[:, K + B:K + K], ["b4", ("SR1", K + B, K + K)], A.min)
    act("b1", 0, B, T.b4[:, 0:B], ["b4"], AF.Relu, -1.0, 16.0)
    tt("DX", 2 * K + B, 3 * K, T.b1[:, 0:B], T.SR1[:, K:K + B], ["b1", ("SR1", K, K + B)], A.min)
    relus(3)
    mins(1, 3)
    act("DX", 2 * K, 2 * K + B, T.UX[:, 0:B], [("UX", 0, B)], AF.Relu)
    moves1_y()
    moves1_z()
    down(1)
    exchange(1)
    dma("s", [("WB1", 512 * me, 512 * me + 512)], [], T.y[:, 512 * me:512 * me + 512], T.WB1[:, 512 * me:512 * me + 512])
    for i, s in enumerate([s for s in range(4) if topo.chip(cores[s]) == topo.chip(core) and s != me] +
                          [s for s in range(4) if topo.chip(cores[s]) != topo.chip(core)]):
        dma("ysy"[i], [("YL", 512 * s, 512 * s + 512)], [], T.y[:, 512 * s:512 * s + 512], T.YL[:, 512 * s:512 * s + 512])
    for sem in sorted(total):
        if known["g"].get(sem, 0) < total[sem]:
            g.wait_ge(T.sem[sem], total[sem])
